import numpy as np
import ml_dtypes


def mxq(x, axis, fmt="e4m3"):
    dtype, down = {"e4m3": (ml_dtypes.float8_e4m3fn, 7), "e5m2": (ml_dtypes.float8_e5m2, 14)}[fmt]
    v = np.moveaxis(np.asarray(x, np.float32).astype(ml_dtypes.bfloat16).astype(np.float64), axis, -1)
    blocks = v.reshape(v.shape[:-1] + (-1, 32))
    amax = np.abs(blocks).max(-1, keepdims=True)
    byte = np.maximum(np.where(amax > 0, np.frexp(amax)[1] - 1 + 127, 0) - down, 1)
    scale = np.exp2(byte - 127.0)
    codes = (blocks / scale).astype(np.float32).astype(dtype).astype(np.float64)
    return np.moveaxis((codes * scale).reshape(v.shape), -1, axis)


WIDE = False


def mx_kscale(k):
    if not WIDE:
        return np.ones(k)
    levels = np.array([10, -10, 5, -5, 0])
    if k % 512:
        return np.exp2(np.random.permutation(np.resize(levels, k // 32))).repeat(32)
    a = np.empty((k // 512, 16))
    for p in range(k // 512):
        a[p, :8] = np.random.permutation(np.resize(levels, 8))
        for g in range(8):
            far = levels[np.abs(levels - a[p, g]) >= 10]
            a[p, g + 8] = far[np.random.randint(len(far))]
    return np.exp2(a.ravel()).repeat(32)


def f64(x):
    return np.asarray(x).astype(np.float64)


def striped(idx):
    return np.tile(np.asarray(idx).reshape(-1, 16).T, (8, 1)).astype(np.uint16)


def unstriped(offs):
    return offs[:16].T.reshape(-1).astype(np.int64)


E2M1 = np.array([0.0, 0.5, 1.0, 1.5, 2.0, 3.0, 4.0, 6.0, -0.0, -0.5, -1.0, -1.5, -2.0, -3.0, -4.0, -6.0])


def pack_weight(w, fmt):
    k, n = w.shape
    w = f64(np.asarray(w, np.float32).astype(ml_dtypes.bfloat16)).reshape(k // 32, 32, n)
    amax = np.abs(w).max(1)
    if fmt == "e4m3":
        byte = np.frexp(amax)[1] - 1 + 127 - 7
    else:
        mant, ex = np.frexp(amax / 6.0)
        byte = np.where(mant > 0.5, ex, ex - 1) + 127
    byte = np.clip(np.where(amax > 0, byte, 1), 1, 254)
    scaled = (w * np.exp2(127.0 - byte)[:, None, :]).reshape(k, n).astype(np.float32)
    by_word = np.ascontiguousarray(scaled.reshape(k // 512, 128, 4, n).transpose(0, 1, 3, 2))
    if fmt == "e4m3":
        words = by_word.astype(ml_dtypes.float8_e4m3fn).view(np.uint8)
    else:
        c = by_word.astype(ml_dtypes.float4_e2m1fn).view(np.uint8) & 0xF
        words = (c[..., 0::2] | (c[..., 1::2] << 4)).reshape(k // 512, 128, 2 * n)
    return np.ascontiguousarray(words), np.ascontiguousarray(byte.astype(np.uint8).reshape(k // 512, 16, n))


def unpack_weight(words, scales, fmt):
    g, _, n = scales.shape
    words = np.ascontiguousarray(words).reshape(g, 128, n, -1)
    if fmt == "e4m3":
        vals = words.view(ml_dtypes.float8_e4m3fn).astype(np.float64)
    else:
        nib = np.empty((g, 128, n, 4), np.uint8)
        nib[..., 0::2] = words & 0xF
        nib[..., 1::2] = words >> 4
        vals = E2M1[nib]
    vals = vals * np.repeat(np.exp2(scales.astype(np.float64) - 127.0), 8, axis=1)[..., None]
    return vals.transpose(0, 1, 3, 2).reshape(g * 512, n)


D, T, I, Q, E, X = 512, 2048, 512, 128, 512, 1024


def setup_inputs():
    n = np.random.standard_normal
    idx = np.random.permutation(T)[:I]
    idx2 = np.random.permutation(T)[:I]
    idx3 = np.random.permutation(X)[:I]
    fd = mx_kscale(D)
    fi = mx_kscale(I)
    keysp = pack_weight(n((D, T)) / fd[:, None], "e4m3")
    return {
        "query": (n((D, Q)) * 1.0 / np.sqrt(D) * fd[:, None]).astype(np.float32),
        "keys_words": keysp[0],
        "keys_scales": keysp[1],
        "os": (np.random.uniform(0.02, 0.08, (1, I)) * fi).astype(np.float32),
        "vals": (n((E, T))).astype(np.float32),
        "vals2": (n((E, X))).astype(np.float32),
        "vsc": (np.random.uniform(0.5, 2.0, (1, I)) / fi).astype(np.float32),
        "offs": striped(idx),
        "offs2": striped(idx2),
        "offs3": striped(idx3),
    }


def reference(query, keys_words, keys_scales, os, vals, vals2, vsc, offs, offs2, offs3):
    idx = unstriped(offs)
    idx2 = unstriped(offs2)
    idx3 = unstriped(offs3)
    keysu = unpack_weight(keys_words, keys_scales, "e4m3")
    queryq = mxq(f64(query), 0, "e4m3")
    a = queryq.T @ keysu
    w = a[:, idx] - a[:, idx2]
    wo1 = w * f64(os)
    wt1 = wo1.T
    vz = np.maximum(f64(vals)[:, idx], f64(vals2)[:, idx3]) * f64(vsc)
    vt1 = vz.T
    wt1q = mxq(wt1, 0, "e4m3")
    vt1q = mxq(vt1, 0, "e4m3")
    o = wt1q.T @ vt1q
    return o

@@ -1,0 +1,176 @@
+from contextlib import ExitStack
+
+import concourse.mybir as mybir
+from concourse.masks import make_identity
+
+D, T, I, Q, E, X = 512, 2048, 512, 128, 512, 1024
+FLOPS = 2 * Q * D * T + 2 * Q * I * E
+
+F32 = mybir.dt.float32
+BF16 = mybir.dt.bfloat16
+I32 = mybir.dt.int32
+U32 = mybir.dt.uint32
+U16 = mybir.dt.uint16
+U8 = mybir.dt.uint8
+FP8X4 = mybir.dt.float8_e4m3fn_x4
+ALU = mybir.AluOpType
+COPY = mybir.ActivationFunctionType.Copy
+
+P = 128
+PACK = 4
+RUN = 8
+BANK = 512
+CHUNKS = T // BANK
+TILES = E // P
+LIST_COLS = I // 16
+VECTOR_COLS = 8
+LAST_VECTOR_COLS = 16
+
+
+def by_place(ap):
+    return ap.rearrange("p (b r j) -> p r b j", r=PACK, j=RUN)
+
+
+def tile_attend_difference_mergedvalues_lean_kernel(
+    tc, query, keys_words, keys_scales, weight_factor, vals, vals2, value_factor, offs, offs2, offs3, out
+):
+    nc = tc.nc
+    with ExitStack() as ctx:
+        keep = ctx.enter_context(tc.tile_pool(name="keep", bufs=1))
+        psum = ctx.enter_context(tc.psum_pool(name="psum", bufs=1))
+
+        list1 = keep.tile([P, LIST_COLS], U16, name="list1")
+        list2 = keep.tile([P, LIST_COLS], U16, name="list2")
+        list3 = keep.tile([P, LIST_COLS], U16, name="list3")
+        store1 = [keep.tile([P, T], F32, name="store1_%d" % n) for n in range(TILES)]
+        store2 = [keep.tile([P, X], F32, name="store2_%d" % n) for n in range(TILES)]
+        q_raw = keep.tile([P, PACK, Q], F32, name="q_raw")
+        k_words = [keep.tile([P, T // 2], I32, name="k_words_%d" % h, align_bytes=64) for h in range(2)]
+        k_scales = keep.tile([P, BANK], U8, name="k_scales", align_bytes=64)
+        factor_rows = keep.tile([P, P], F32, name="factor_rows")
+        ident = keep.tile([P, P], F32, name="ident")
+
+        def load_values(n):
+            rows = slice(n * P, (n + 1) * P)
+            nc.sync.dma_start(store1[n][:], vals[rows, :])
+            nc.sync.dma_start(store2[n][:], vals2[rows, :])
+
+        first_row = P - 2 * PACK
+        nc.gpsimd.memset(factor_rows[0:first_row, :], 0.0)
+        make_identity(nc, ident[:])
+
+        def load_keys(h):
+            tokens = slice(h * T // 2, (h + 1) * T // 2)
+            nc.sync.dma_start(k_words[h][:], keys_words[0, :, tokens, :].rearrange("p n t -> p (n t)").bitcast(I32))
+
+        nc.sync.dma_start(list1[:], offs)
+        nc.sync.dma_start(q_raw[:], query.rearrange("(p t) q -> p t q", t=PACK))
+        load_keys(0)
+        for quad in range(4):
+            nc.sync.dma_start(
+                k_scales[32 * quad : 32 * quad + 4 * CHUNKS, :].bitcast(I32),
+                keys_scales[0, 4 * quad : 4 * quad + 4, :].bitcast(I32).rearrange("r (c n) -> c r n", c=CHUNKS),
+            )
+        load_keys(1)
+        nc.sync.dma_start(list2[:], offs2)
+        nc.sync.dma_start(store1[0][:], vals[0:P, :])
+        nc.sync.dma_start(list3[:], offs3)
+        nc.sync.dma_start(store2[0][:], vals2[0:P, :])
+        for n, factor in enumerate((weight_factor, value_factor)):
+            nc.sync.dma_start(
+                factor_rows[first_row + PACK * n : first_row + PACK * (n + 1), :].rearrange("r (b j) -> r b j", j=RUN),
+                factor[0].rearrange("(b r j) -> r b j", r=PACK, j=RUN),
+            )
+        for n in range(1, TILES):
+            load_values(n)
+
+        def quantise(src, name):
+            codes = keep.tile([P, P], U32, name=name + "_codes", align_bytes=64)
+            scales = keep.tile([P, P], U8, name=name + "_scales", align_bytes=64)
+            nc.vector.quantize_mx(codes[:].bitcast(FP8X4), scales[:], src[:].rearrange("p c t -> p (c t)"))
+            return codes, scales
+
+        def turn_scale_quantise(src, factor, name):
+            bank = psum.tile([P, PACK, P], F32, name=name + "_bank", tag="turn", bufs=4)
+            for r in range(PACK):
+                nc.tensor.transpose(bank[:, r, :], src[:, r * P : (r + 1) * P], ident[:])
+            woven = keep.tile([P, P, PACK], BF16, name=name + "_woven", align_bytes=64)
+            nc.vector.tensor_tensor(
+                woven[:],
+                bank[:].rearrange("p r c -> p c r"),
+                factor.unsqueeze(1).to_broadcast([P, P, PACK]),
+                ALU.mult,
+            )
+            return quantise(woven, name)
+
+        def gather(window, offsets, name, vector_cols):
+            picked = keep.tile([P, I], F32, name=name)
+            cut = 16 * vector_cols
+            nc.vector.tensor_copy(picked[:, :cut], window[:].indirect(offsets[:, :vector_cols]))
+            nc.scalar.activation(picked[:, cut:], window[:].indirect(offsets[:, vector_cols:]), COPY)
+            return picked
+
+        def combine(left, right, op, name):
+            merged = keep.tile([P, I], F32, name=name)
+            placed = merged[:].rearrange("p (r b j) -> p r b j", r=PACK, j=RUN)
+            for pair in (slice(0, 2), slice(2, 4)):
+                nc.vector.tensor_tensor(placed[:, pair], by_place(left[:])[:, pair], by_place(right[:])[:, pair], op)
+            return merged
+
+        def values_operand(n):
+            vector_cols = LAST_VECTOR_COLS if n == TILES - 1 else VECTOR_COLS
+            picked1 = gather(store1[n], list1, "picked1_%d" % n, VECTOR_COLS)
+            picked2 = gather(store2[n], list3, "picked2_%d" % n, vector_cols)
+            larger = combine(picked1, picked2, ALU.max, "larger_%d" % n)
+            return turn_scale_quantise(larger, factors[:, PACK : 2 * PACK], "v%d" % n)
+
+        q_woven = keep.tile([P, Q, PACK], BF16, name="q_woven", align_bytes=64)
+        nc.vector.tensor_copy(q_woven[:], q_raw[:].rearrange("p t q -> p q t"))
+        q_codes, q_scales = quantise(q_woven, "q")
+
+        scores = keep.tile([P, T], F32, name="scores")
+        for c in range(CHUNKS):
+            cols = slice(c * BANK, (c + 1) * BANK)
+            score_bank = psum.tile([P, BANK], F32, name="score_bank", tag="score", bufs=4)
+            nc.tensor.matmul_mx(
+                score_bank[:],
+                lhsT=q_codes[:].bitcast(FP8X4),
+                lhsT_scale=q_scales[:],
+                rhs=k_words[c // 2][:, (c % 2) * BANK : (c % 2 + 1) * BANK].bitcast(FP8X4),
+                rhs_scale=k_scales[4 * c : P, :],
+                start=True,
+                stop=True,
+            )
+            if c % 2 == 0:
+                nc.vector.tensor_copy(scores[:, cols], score_bank[:])
+            else:
+                nc.scalar.copy(scores[:, cols], score_bank[:])
+
+        factor_bank = psum.tile([P, P], F32, name="factor_bank", tag="turn", bufs=4)
+        nc.tensor.transpose(factor_bank[:], factor_rows[:], ident[:])
+        factors = keep.tile([P, 2 * PACK], F32, name="factors")
+        nc.scalar.copy(factors[:], factor_bank[:, first_row:P])
+
+        first = gather(scores, list1, "first", VECTOR_COLS)
+        second = gather(scores, list2, "second", VECTOR_COLS)
+        diff = combine(first, second, ALU.subtract, "diff")
+        w_codes, w_scales = turn_scale_quantise(diff, factors[:, 0:PACK], "w")
+
+        for n in range(TILES):
+            v_codes, v_scales = values_operand(n)
+            out_bank = psum.tile([P, P], F32, name="out_bank", tag="score", bufs=4)
+            nc.tensor.matmul_mx(
+                out_bank[:],
+                lhsT=w_codes[:].bitcast(FP8X4),
+                lhsT_scale=w_scales[:],
+                rhs=v_codes[:].bitcast(FP8X4),
+                rhs_scale=v_scales[:],
+                start=True,
+                stop=True,
+            )
+            result = keep.tile([P, P], F32, name="result_%d" % n)
+            if n == TILES - 1:
+                nc.scalar.copy(result[:], out_bank[:])
+            else:
+                nc.vector.tensor_copy(result[:], out_bank[:])
+            nc.sync.dma_start(out[:, n * P : (n + 1) * P], result[:])

@@ -23,8 +23,8 @@ BANK = 512
 CHUNKS = T // BANK
 TILES = E // P
 LIST_COLS = I // 16
-VECTOR_COLS = 8
-LAST_VECTOR_COLS = 16
+FIRST_STORE_VECTOR_COLS = (16, 0, 8, 0)
+SECOND_STORE_VECTOR_COLS = (0, 0, 0, 18)
 
 
 def by_place(ap):
@@ -47,91 +47,100 @@ def tile_attend_difference_mergedvalues_lean_kernel(
         q_raw = keep.tile([P, PACK, Q], F32, name="q_raw")
         k_words = [keep.tile([P, T // 2], I32, name="k_words_%d" % h, align_bytes=64) for h in range(2)]
         k_scales = keep.tile([P, BANK], U8, name="k_scales", align_bytes=64)
-        factor_rows = keep.tile([P, P], F32, name="factor_rows")
+        factor_rows = keep.tile([2, I], F32, name="factor_rows")
         ident = keep.tile([P, P], F32, name="ident")
 
-        def load_values(n):
-            rows = slice(n * P, (n + 1) * P)
-            nc.sync.dma_start(store1[n][:], vals[rows, :])
-            nc.sync.dma_start(store2[n][:], vals2[rows, :])
+        factor_placed = keep.tile([P, I], F32, name="factor_placed")
 
-        first_row = P - 2 * PACK
-        nc.gpsimd.memset(factor_rows[0:first_row, :], 0.0)
+        def load_store1(n):
+            nc.sync.dma_start(store1[n][:], vals[n * P : (n + 1) * P, :])
+
+        def load_store2(n):
+            nc.sync.dma_start(store2[n][:], vals2[n * P : (n + 1) * P, :])
+
         make_identity(nc, ident[:])
+        nc.gpsimd.memset(factor_placed[:], 0.0)
 
         def load_keys(h):
             tokens = slice(h * T // 2, (h + 1) * T // 2)
             nc.sync.dma_start(k_words[h][:], keys_words[0, :, tokens, :].rearrange("p n t -> p (n t)").bitcast(I32))
 
-        nc.sync.dma_start(list1[:], offs)
         nc.sync.dma_start(q_raw[:], query.rearrange("(p t) q -> p t q", t=PACK))
-        load_keys(0)
         for quad in range(4):
             nc.sync.dma_start(
                 k_scales[32 * quad : 32 * quad + 4 * CHUNKS, :].bitcast(I32),
                 keys_scales[0, 4 * quad : 4 * quad + 4, :].bitcast(I32).rearrange("r (c n) -> c r n", c=CHUNKS),
             )
+        load_keys(0)
         load_keys(1)
-        nc.sync.dma_start(list2[:], offs2)
-        nc.sync.dma_start(store1[0][:], vals[0:P, :])
+        load_store2(0)
         nc.sync.dma_start(list3[:], offs3)
-        nc.sync.dma_start(store2[0][:], vals2[0:P, :])
-        for n, factor in enumerate((weight_factor, value_factor)):
-            nc.sync.dma_start(
-                factor_rows[first_row + PACK * n : first_row + PACK * (n + 1), :].rearrange("r (b j) -> r b j", j=RUN),
-                factor[0].rearrange("(b r j) -> r b j", r=PACK, j=RUN),
-            )
-        for n in range(1, TILES):
-            load_values(n)
+        nc.sync.dma_start(list1[:], offs)
+        nc.sync.dma_start(list2[:], offs2)
+        nc.sync.dma_start(factor_rows[0:1, :], weight_factor)
+        nc.sync.dma_start(factor_rows[1:2, :], value_factor)
+        load_store1(0)
+        for n in range(1, TILES - 1):
+            load_store2(n)
+            load_store1(n)
+        load_store1(TILES - 1)
+        load_store2(TILES - 1)
 
-        def quantise(src, name):
-            codes = keep.tile([P, P], U32, name=name + "_codes", align_bytes=64)
-            scales = keep.tile([P, P], U8, name=name + "_scales", align_bytes=64)
+        def quantise(src, name, tag):
+            width = src.shape[1]
+            codes = keep.tile([P, width], U32, name="codes", tag=tag, align_bytes=64)
+            scales = keep.tile([P, width], U8, name=name + "_scales", align_bytes=64)
             nc.vector.quantize_mx(codes[:].bitcast(FP8X4), scales[:], src[:].rearrange("p c t -> p (c t)"))
             return codes, scales
 
-        def turn_scale_quantise(src, factor, name):
-            bank = psum.tile([P, PACK, P], F32, name=name + "_bank", tag="turn", bufs=4)
+        def gather(window, offsets, tag, vector_cols):
+            picked = keep.tile([P, I], F32, name="picked", tag=tag, align_bytes=64)
+            cut = 16 * vector_cols
+            if vector_cols:
+                nc.vector.tensor_copy(picked[:, :cut], window[:].indirect(offsets[:, :vector_cols]))
+            if vector_cols < LIST_COLS:
+                nc.scalar.activation(picked[:, cut:], window[:].indirect(offsets[:, vector_cols:]), COPY)
+            return picked
+
+        def placed_view(ap):
+            return ap.rearrange("p (r b j) -> p r b j", r=PACK, j=RUN)
+
+        def turn(placed, tag):
+            bank = psum.tile([P, PACK, P], F32, name="turn_bank", tag=tag)
             for r in range(PACK):
-                nc.tensor.transpose(bank[:, r, :], src[:, r * P : (r + 1) * P], ident[:])
-            woven = keep.tile([P, P, PACK], BF16, name=name + "_woven", align_bytes=64)
+                nc.tensor.transpose(bank[:, r, :], placed[:, r * P : (r + 1) * P], ident[:])
+            return bank
+
+        def combine_and_turn(left, right, op, name, places, bank_tag):
+            merged = keep.tile([P, I], F32, name=name)
+            for r in range(0, PACK, places):
+                part = slice(r, r + places)
+                nc.vector.tensor_tensor(
+                    placed_view(merged[:])[:, part], by_place(left[:])[:, part], by_place(right[:])[:, part], op
+                )
+            return turn(merged, bank_tag)
+
+        def scale_and_weave(bank, factor, woven):
             nc.vector.tensor_tensor(
-                woven[:],
+                woven,
                 bank[:].rearrange("p r c -> p c r"),
                 factor.unsqueeze(1).to_broadcast([P, P, PACK]),
                 ALU.mult,
             )
-            return quantise(woven, name)
 
-        def gather(window, offsets, name, vector_cols):
-            picked = keep.tile([P, I], F32, name=name)
-            cut = 16 * vector_cols
-            nc.vector.tensor_copy(picked[:, :cut], window[:].indirect(offsets[:, :vector_cols]))
-            nc.scalar.activation(picked[:, cut:], window[:].indirect(offsets[:, vector_cols:]), COPY)
-            return picked
-
-        def combine(left, right, op, name):
-            merged = keep.tile([P, I], F32, name=name)
-            placed = merged[:].rearrange("p (r b j) -> p r b j", r=PACK, j=RUN)
-            for pair in (slice(0, 2), slice(2, 4)):
-                nc.vector.tensor_tensor(placed[:, pair], by_place(left[:])[:, pair], by_place(right[:])[:, pair], op)
-            return merged
-
-        def values_operand(n):
-            vector_cols = LAST_VECTOR_COLS if n == TILES - 1 else VECTOR_COLS
-            picked1 = gather(store1[n], list1, "picked1_%d" % n, VECTOR_COLS)
-            picked2 = gather(store2[n], list3, "picked2_%d" % n, vector_cols)
-            larger = combine(picked1, picked2, ALU.max, "larger_%d" % n)
-            return turn_scale_quantise(larger, factors[:, PACK : 2 * PACK], "v%d" % n)
+        def turn_values(n):
+            picked1 = gather(store1[n], list1, "from1_%d" % n, FIRST_STORE_VECTOR_COLS[n])
+            picked2 = gather(store2[n], list3, "from2_%d" % n, SECOND_STORE_VECTOR_COLS[n])
+            return combine_and_turn(picked1, picked2, ALU.max, "larger_%d" % n, 1, "turn_%d" % n)
 
         q_woven = keep.tile([P, Q, PACK], BF16, name="q_woven", align_bytes=64)
         nc.vector.tensor_copy(q_woven[:], q_raw[:].rearrange("p t q -> p q t"))
-        q_codes, q_scales = quantise(q_woven, "q")
+        q_codes, q_scales = quantise(q_woven, "q", "q_codes")
 
         scores = keep.tile([P, T], F32, name="scores")
         for c in range(CHUNKS):
             cols = slice(c * BANK, (c + 1) * BANK)
-            score_bank = psum.tile([P, BANK], F32, name="score_bank", tag="score", bufs=4)
+            score_bank = psum.tile([P, BANK], F32, name="score_bank", tag="score_%d" % c)
             nc.tensor.matmul_mx(
                 score_bank[:],
                 lhsT=q_codes[:].bitcast(FP8X4),
@@ -141,26 +150,22 @@ def tile_attend_difference_mergedvalues_lean_kernel(
                 start=True,
                 stop=True,
             )
-            if c % 2 == 0:
-                nc.vector.tensor_copy(scores[:, cols], score_bank[:])
-            else:
-                nc.scalar.copy(scores[:, cols], score_bank[:])
+            copy = nc.vector.tensor_copy if c % 2 == 0 else nc.scalar.copy
+            copy(scores[:, cols], score_bank[:])
 
-        factor_bank = psum.tile([P, P], F32, name="factor_bank", tag="turn", bufs=4)
-        nc.tensor.transpose(factor_bank[:], factor_rows[:], ident[:])
-        factors = keep.tile([P, 2 * PACK], F32, name="factors")
-        nc.scalar.copy(factors[:], factor_bank[:, first_row:P])
+        nc.gpsimd.tensor_copy(placed_view(factor_placed[0:2, :]), by_place(factor_rows[:]))
+        factor_bank = turn(factor_placed, "score_%d" % (CHUNKS - 1))
+        factors = keep.tile([P, 2, PACK], F32, name="factors")
+        nc.vector.tensor_copy(factors[:], factor_bank[:, :, 0:2].rearrange("p r f -> p f r"))
 
-        first = gather(scores, list1, "first", VECTOR_COLS)
-        second = gather(scores, list2, "second", VECTOR_COLS)
-        diff = combine(first, second, ALU.subtract, "diff")
-        w_codes, w_scales = turn_scale_quantise(diff, factors[:, 0:PACK], "w")
+        first = gather(scores, list1, "first", LIST_COLS)
+        second = gather(scores, list2, "second", 0)
+        w_bank = combine_and_turn(first, second, ALU.subtract, "diff", PACK, "score_0")
 
-        for n in range(TILES):
-            v_codes, v_scales = values_operand(n)
-            out_bank = psum.tile([P, P], F32, name="out_bank", tag="score", bufs=4)
+        def multiply(v_codes, v_scales, tag):
+            bank = psum.tile([P, v_codes.shape[1]], F32, name="out_bank", tag=tag)
             nc.tensor.matmul_mx(
-                out_bank[:],
+                bank[:],
                 lhsT=w_codes[:].bitcast(FP8X4),
                 lhsT_scale=w_scales[:],
                 rhs=v_codes[:].bitcast(FP8X4),
@@ -168,9 +173,36 @@ def tile_attend_difference_mergedvalues_lean_kernel(
                 start=True,
                 stop=True,
             )
-            result = keep.tile([P, P], F32, name="result_%d" % n)
-            if n == TILES - 1:
-                nc.scalar.copy(result[:], out_bank[:])
-            else:
-                nc.vector.tensor_copy(result[:], out_bank[:])
-            nc.sync.dma_start(out[:, n * P : (n + 1) * P], result[:])
+            return bank
+
+        def store(bank, first_col, tag, queue):
+            width = bank.shape[1]
+            result = keep.tile([P, width], F32, name="result", tag=tag, align_bytes=64)
+            nc.scalar.copy(result[:], bank[:])
+            queue.dma_start(out[:, first_col : first_col + width], result[:])
+
+        def woven_tile(width, tag):
+            return keep.tile([P, width, PACK], BF16, name="woven", tag=tag, align_bytes=64)
+
+        weight_places, value_places = factors[:, 0, :], factors[:, 1, :]
+        v_bank0 = turn_values(0)
+        w_woven = woven_tile(Q, "from1_0")
+        scale_and_weave(w_bank, weight_places, w_woven[:])
+        woven01 = woven_tile(2 * P, "woven_01")
+        scale_and_weave(v_bank0, value_places, woven01[:, 0:P, :])
+
+        v_bank1 = turn_values(1)
+        w_codes, w_scales = quantise(w_woven, "w", "from1_1")
+        scale_and_weave(v_bank1, value_places, woven01[:, P : 2 * P, :])
+
+        v_bank2 = turn_values(2)
+        out01 = multiply(*quantise(woven01, "v01", "from1_2"), "score_1")
+        woven2 = woven_tile(P, "woven_2")
+        scale_and_weave(v_bank2, value_places, woven2[:])
+
+        v_bank3 = turn_values(3)
+        store(out01, 0, "from2_3", nc.sync)
+        store(multiply(*quantise(woven2, "v2", "from1_3"), "score_2"), 2 * P, "result_2", nc.sync)
+        woven3 = woven_tile(P, "woven_3")
+        scale_and_weave(v_bank3, value_places, woven3[:])
+        store(multiply(*quantise(woven3, "v3", "codes_3"), "score_3"), 3 * P, "result_3", nc.scalar)

@@ -23,7 +23,7 @@ BANK = 512
 CHUNKS = T // BANK
 TILES = E // P
 LIST_COLS = I // 16
-FIRST_STORE_VECTOR_COLS = (16, 0, 8, 0)
+FIRST_STORE_VECTOR_COLS = (0, 0, 14, 0)
 SECOND_STORE_VECTOR_COLS = (0, 0, 0, 18)
 
 
@@ -65,6 +65,8 @@ def tile_attend_difference_mergedvalues_lean_kernel(
             tokens = slice(h * T // 2, (h + 1) * T // 2)
             nc.sync.dma_start(k_words[h][:], keys_words[0, :, tokens, :].rearrange("p n t -> p (n t)").bitcast(I32))
 
+        nc.sync.dma_start(factor_rows[0:1, :], weight_factor)
+        nc.sync.dma_start(factor_rows[1:2, :], value_factor)
         nc.sync.dma_start(q_raw[:], query.rearrange("(p t) q -> p t q", t=PACK))
         for quad in range(4):
             nc.sync.dma_start(
@@ -77,8 +79,6 @@ def tile_attend_difference_mergedvalues_lean_kernel(
         nc.sync.dma_start(list3[:], offs3)
         nc.sync.dma_start(list1[:], offs)
         nc.sync.dma_start(list2[:], offs2)
-        nc.sync.dma_start(factor_rows[0:1, :], weight_factor)
-        nc.sync.dma_start(factor_rows[1:2, :], value_factor)
         load_store1(0)
         for n in range(1, TILES - 1):
             load_store2(n)
@@ -129,9 +129,11 @@ def tile_attend_difference_mergedvalues_lean_kernel(
             )
 
         def turn_values(n):
-            picked1 = gather(store1[n], list1, "from1_%d" % n, FIRST_STORE_VECTOR_COLS[n])
             picked2 = gather(store2[n], list3, "from2_%d" % n, SECOND_STORE_VECTOR_COLS[n])
+            picked1 = gather(store1[n], list1, "from1_%d" % n, FIRST_STORE_VECTOR_COLS[n])
             return combine_and_turn(picked1, picked2, ALU.max, "larger_%d" % n, 1, "turn_%d" % n)
+
+        nc.vector.tensor_copy(placed_view(factor_placed[0:2, :]), by_place(factor_rows[:]))
 
         q_woven = keep.tile([P, Q, PACK], BF16, name="q_woven", align_bytes=64)
         nc.vector.tensor_copy(q_woven[:], q_raw[:].rearrange("p t q -> p q t"))
@@ -150,13 +152,12 @@ def tile_attend_difference_mergedvalues_lean_kernel(
                 start=True,
                 stop=True,
             )
-            copy = nc.vector.tensor_copy if c % 2 == 0 else nc.scalar.copy
+            copy = nc.scalar.copy if c == 1 else nc.vector.tensor_copy
             copy(scores[:, cols], score_bank[:])
 
-        nc.gpsimd.tensor_copy(placed_view(factor_placed[0:2, :]), by_place(factor_rows[:]))
         factor_bank = turn(factor_placed, "score_%d" % (CHUNKS - 1))
         factors = keep.tile([P, 2, PACK], F32, name="factors")
-        nc.vector.tensor_copy(factors[:], factor_bank[:, :, 0:2].rearrange("p r f -> p f r"))
+        nc.scalar.copy(factors[:], factor_bank[:, :, 0:2].rearrange("p r f -> p f r"))
 
         first = gather(scores, list1, "first", LIST_COLS)
         second = gather(scores, list2, "second", 0)

from contextlib import ExitStack

import concourse.mybir as mybir
from concourse.masks import make_identity

D, T, I, Q, E, X = 512, 2048, 512, 128, 512, 1024
FLOPS = 2 * Q * D * T + 2 * Q * I * E

F32 = mybir.dt.float32
BF16 = mybir.dt.bfloat16
I32 = mybir.dt.int32
U32 = mybir.dt.uint32
U16 = mybir.dt.uint16
U8 = mybir.dt.uint8
FP8X4 = mybir.dt.float8_e4m3fn_x4
ALU = mybir.AluOpType
COPY = mybir.ActivationFunctionType.Copy

P = 128
PACK = 4
RUN = 8
BANK = 512
CHUNKS = T // BANK
TILES = E // P
LIST_COLS = I // 16
FIRST_STORE_VECTOR_COLS = (0, 0, 14, 0)
SECOND_STORE_VECTOR_COLS = (0, 0, 0, 18)


def by_place(ap):
    return ap.rearrange("p (b r j) -> p r b j", r=PACK, j=RUN)


def tile_attend_difference_mergedvalues_lean_kernel(
    tc, query, keys_words, keys_scales, weight_factor, vals, vals2, value_factor, offs, offs2, offs3, out
):
    nc = tc.nc
    with ExitStack() as ctx:
        keep = ctx.enter_context(tc.tile_pool(name="keep", bufs=1))
        psum = ctx.enter_context(tc.psum_pool(name="psum", bufs=1))

        list1 = keep.tile([P, LIST_COLS], U16, name="list1")
        list2 = keep.tile([P, LIST_COLS], U16, name="list2")
        list3 = keep.tile([P, LIST_COLS], U16, name="list3")
        store1 = [keep.tile([P, T], F32, name="store1_%d" % n) for n in range(TILES)]
        store2 = [keep.tile([P, X], F32, name="store2_%d" % n) for n in range(TILES)]
        q_raw = keep.tile([P, PACK, Q], F32, name="q_raw")
        k_words = [keep.tile([P, T // 2], I32, name="k_words_%d" % h, align_bytes=64) for h in range(2)]
        k_scales = keep.tile([P, BANK], U8, name="k_scales", align_bytes=64)
        factor_rows = keep.tile([2, I], F32, name="factor_rows")
        ident = keep.tile([P, P], F32, name="ident")

        factor_placed = keep.tile([P, I], F32, name="factor_placed")

        def load_store1(n):
            nc.sync.dma_start(store1[n][:], vals[n * P : (n + 1) * P, :])

        def load_store2(n):
            nc.sync.dma_start(store2[n][:], vals2[n * P : (n + 1) * P, :])

        make_identity(nc, ident[:])
        nc.gpsimd.memset(factor_placed[:], 0.0)

        def load_keys(h):
            tokens = slice(h * T // 2, (h + 1) * T // 2)
            nc.sync.dma_start(k_words[h][:], keys_words[0, :, tokens, :].rearrange("p n t -> p (n t)").bitcast(I32))

        nc.sync.dma_start(factor_rows[0:1, :], weight_factor)
        nc.sync.dma_start(factor_rows[1:2, :], value_factor)
        nc.sync.dma_start(q_raw[:], query.rearrange("(p t) q -> p t q", t=PACK))
        for quad in range(4):
            nc.sync.dma_start(
                k_scales[32 * quad : 32 * quad + 4 * CHUNKS, :].bitcast(I32),
                keys_scales[0, 4 * quad : 4 * quad + 4, :].bitcast(I32).rearrange("r (c n) -> c r n", c=CHUNKS),
            )
        load_keys(0)
        load_keys(1)
        load_store2(0)
        nc.sync.dma_start(list3[:], offs3)
        nc.sync.dma_start(list1[:], offs)
        nc.sync.dma_start(list2[:], offs2)
        load_store1(0)
        for n in range(1, TILES - 1):
            load_store2(n)
            load_store1(n)
        load_store1(TILES - 1)
        load_store2(TILES - 1)

        def quantise(src, name, tag):
            width = src.shape[1]
            codes = keep.tile([P, width], U32, name="codes", tag=tag, align_bytes=64)
            scales = keep.tile([P, width], U8, name=name + "_scales", align_bytes=64)
            nc.vector.quantize_mx(codes[:].bitcast(FP8X4), scales[:], src[:].rearrange("p c t -> p (c t)"))
            return codes, scales

        def gather(window, offsets, tag, vector_cols):
            picked = keep.tile([P, I], F32, name="picked", tag=tag, align_bytes=64)
            cut = 16 * vector_cols
            if vector_cols:
                nc.vector.tensor_copy(picked[:, :cut], window[:].indirect(offsets[:, :vector_cols]))
            if vector_cols < LIST_COLS:
                nc.scalar.activation(picked[:, cut:], window[:].indirect(offsets[:, vector_cols:]), COPY)
            return picked

        def placed_view(ap):
            return ap.rearrange("p (r b j) -> p r b j", r=PACK, j=RUN)

        def turn(placed, tag):
            bank = psum.tile([P, PACK, P], F32, name="turn_bank", tag=tag)
            for r in range(PACK):
                nc.tensor.transpose(bank[:, r, :], placed[:, r * P : (r + 1) * P], ident[:])
            return bank

        def combine_and_turn(left, right, op, name, places, bank_tag):
            merged = keep.tile([P, I], F32, name=name)
            for r in range(0, PACK, places):
                part = slice(r, r + places)
                nc.vector.tensor_tensor(
                    placed_view(merged[:])[:, part], by_place(left[:])[:, part], by_place(right[:])[:, part], op
                )
            return turn(merged, bank_tag)

        def scale_and_weave(bank, factor, woven):
            nc.vector.tensor_tensor(
                woven,
                bank[:].rearrange("p r c -> p c r"),
                factor.unsqueeze(1).to_broadcast([P, P, PACK]),
                ALU.mult,
            )

        def turn_values(n):
            picked2 = gather(store2[n], list3, "from2_%d" % n, SECOND_STORE_VECTOR_COLS[n])
            picked1 = gather(store1[n], list1, "from1_%d" % n, FIRST_STORE_VECTOR_COLS[n])
            return combine_and_turn(picked1, picked2, ALU.max, "larger_%d" % n, 1, "turn_%d" % n)

        nc.vector.tensor_copy(placed_view(factor_placed[0:2, :]), by_place(factor_rows[:]))

        q_woven = keep.tile([P, Q, PACK], BF16, name="q_woven", align_bytes=64)
        nc.vector.tensor_copy(q_woven[:], q_raw[:].rearrange("p t q -> p q t"))
        q_codes, q_scales = quantise(q_woven, "q", "q_codes")

        scores = keep.tile([P, T], F32, name="scores")
        for c in range(CHUNKS):
            cols = slice(c * BANK, (c + 1) * BANK)
            score_bank = psum.tile([P, BANK], F32, name="score_bank", tag="score_%d" % c)
            nc.tensor.matmul_mx(
                score_bank[:],
                lhsT=q_codes[:].bitcast(FP8X4),
                lhsT_scale=q_scales[:],
                rhs=k_words[c // 2][:, (c % 2) * BANK : (c % 2 + 1) * BANK].bitcast(FP8X4),
                rhs_scale=k_scales[4 * c : P, :],
                start=True,
                stop=True,
            )
            copy = nc.scalar.copy if c == 1 else nc.vector.tensor_copy
            copy(scores[:, cols], score_bank[:])

        factor_bank = turn(factor_placed, "score_%d" % (CHUNKS - 1))
        factors = keep.tile([P, 2, PACK], F32, name="factors")
        nc.scalar.copy(factors[:], factor_bank[:, :, 0:2].rearrange("p r f -> p f r"))

        first = gather(scores, list1, "first", LIST_COLS)
        second = gather(scores, list2, "second", 0)
        w_bank = combine_and_turn(first, second, ALU.subtract, "diff", PACK, "score_0")

        def multiply(v_codes, v_scales, tag):
            bank = psum.tile([P, v_codes.shape[1]], F32, name="out_bank", tag=tag)
            nc.tensor.matmul_mx(
                bank[:],
                lhsT=w_codes[:].bitcast(FP8X4),
                lhsT_scale=w_scales[:],
                rhs=v_codes[:].bitcast(FP8X4),
                rhs_scale=v_scales[:],
                start=True,
                stop=True,
            )
            return bank

        def store(bank, first_col, tag, queue):
            width = bank.shape[1]
            result = keep.tile([P, width], F32, name="result", tag=tag, align_bytes=64)
            nc.scalar.copy(result[:], bank[:])
            queue.dma_start(out[:, first_col : first_col + width], result[:])

        def woven_tile(width, tag):
            return keep.tile([P, width, PACK], BF16, name="woven", tag=tag, align_bytes=64)

        weight_places, value_places = factors[:, 0, :], factors[:, 1, :]
        v_bank0 = turn_values(0)
        w_woven = woven_tile(Q, "from1_0")
        scale_and_weave(w_bank, weight_places, w_woven[:])
        woven01 = woven_tile(2 * P, "woven_01")
        scale_and_weave(v_bank0, value_places, woven01[:, 0:P, :])

        v_bank1 = turn_values(1)
        w_codes, w_scales = quantise(w_woven, "w", "from1_1")
        scale_and_weave(v_bank1, value_places, woven01[:, P : 2 * P, :])

        v_bank2 = turn_values(2)
        out01 = multiply(*quantise(woven01, "v01", "from1_2"), "score_1")
        woven2 = woven_tile(P, "woven_2")
        scale_and_weave(v_bank2, value_places, woven2[:])

        v_bank3 = turn_values(3)
        store(out01, 0, "from2_3", nc.sync)
        store(multiply(*quantise(woven2, "v2", "from1_3"), "score_2"), 2 * P, "result_2", nc.sync)
        woven3 = woven_tile(P, "woven_3")
        scale_and_weave(v_bank3, value_places, woven3[:])
        store(multiply(*quantise(woven3, "v3", "codes_3"), "score_3"), 3 * P, "result_3", nc.scalar)
